import numpy as np
import ml_dtypes


def mxq(x, axis, fmt="e4m3"):
    dtype, down = {"e4m3": (ml_dtypes.float8_e4m3fn, 7), "e5m2": (ml_dtypes.float8_e5m2, 14)}[fmt]
    v = np.moveaxis(np.asarray(x, np.float32).astype(ml_dtypes.bfloat16).astype(np.float64), axis, -1)
    blocks = v.reshape(v.shape[:-1] + (-1, 32))
    amax = np.abs(blocks).max(-1, keepdims=True)
    byte = np.maximum(np.where(amax > 0, np.frexp(amax)[1] - 1 + 127, 0) - down, 1)
    scale = np.exp2(byte - 127.0)
    codes = (blocks / scale).astype(np.float32).astype(dtype).astype(np.float64)
    return np.moveaxis((codes * scale).reshape(v.shape), -1, axis)


WIDE = False


def mx_kscale(k):
    if not WIDE:
        return np.ones(k)
    levels = np.array([10, -10, 5, -5, 0])
    if k % 512:
        return np.exp2(np.random.permutation(np.resize(levels, k // 32))).repeat(32)
    a = np.empty((k // 512, 16))
    for p in range(k // 512):
        a[p, :8] = np.random.permutation(np.resize(levels, 8))
        for g in range(8):
            far = levels[np.abs(levels - a[p, g]) >= 10]
            a[p, g + 8] = far[np.random.randint(len(far))]
    return np.exp2(a.ravel()).repeat(32)


def f64(x):
    return np.asarray(x).astype(np.float64)


def striped(idx):
    return np.tile(idx.reshape(-1, 16).T, (8, 1)).astype(np.uint16)


def unstriped(offs):
    return offs[:16].T.reshape(-1).astype(np.int64)


def relu(v):
    return np.maximum(v, 0.0)


K, T, E, C, H, N = 1536, 1024, 2, 256, 512, 128


def by_expert(wq, xq):
    return np.concatenate([wq[e].T @ xq[:, e * C:(e + 1) * C] for e in range(E)], axis=1)


def setup_inputs():
    n = np.random.standard_normal
    s = mx_kscale(K)[:, None]
    u = mx_kscale(H)
    return {
        "xT": (n((K, T)) * s).astype(np.float32),
        "w1": (n((E, K, H)) / np.sqrt(K) / s[None]).astype(np.float32),
        "w3": (n((E, K, H)) / np.sqrt(K) / s[None] * u[None, None, :]).astype(np.float32),
        "w2": (n((E, H, N)) / np.sqrt(H) / u[None, :, None]).astype(np.float32),
        "gate": np.tile(np.random.uniform(0.2, 1.0, E * C), (N, 1)).astype(np.float32),
        "offs": striped(np.random.permutation(T)[:E * C]),
    }


def reference(xT, w1, w3, w2, gate, offs):
    idx = unstriped(offs)
    xq = mxq(f64(xT)[:, idx], 0, "e4m3")
    h = relu(by_expert(mxq(f64(w1), 1, "e4m3"), xq))
    h = h * by_expert(mxq(f64(w3), 1, "e4m3"), xq)
    y = by_expert(mxq(f64(w2), 1, "e4m3"), mxq(h, 0, "e4m3"))
    out = np.zeros((N, T))
    out[:, idx] = f64(gate) * y
    return out

@@ -1,0 +1,179 @@
+from contextlib import ExitStack
+
+import concourse.mybir as mybir
+
+K, T, E, C, H, N = 1536, 1024, 2, 256, 512, 128
+FLOPS = 2 * E * C * (2 * K * H + H * N)
+
+F32 = mybir.dt.float32
+BF16 = mybir.dt.bfloat16
+U32 = mybir.dt.uint32
+U16 = mybir.dt.uint16
+U8 = mybir.dt.uint8
+FP8X4 = mybir.dt.float8_e4m3fn_x4
+MULT = mybir.AluOpType.mult
+RELU = mybir.ActivationFunctionType.Relu
+
+P = 128
+J = 4
+PASS = P * J
+PASSES = K // PASS
+SLOTS = E * C
+HALF_T = T // 2
+GROUP = 128
+
+X_CUT = 384
+W_CUT = 64
+L_CUT = 24
+
+
+def tile_routed_moe_kernel(tc, xT, w1, w3, w2, gate, offs, out):
+    nc = tc.nc
+    xT_view = xT.rearrange("(g p j) n -> g p j n", p=P, j=J)
+    w_views = [w.rearrange("e (g p j) n -> e g p j n", p=P, j=J) for w in (w1, w3)]
+    w2_view = w2.rearrange("e (p j) n -> e p j n", j=J)
+    with ExitStack() as ctx:
+        keep = ctx.enter_context(tc.tile_pool(name="keep", bufs=1))
+        raws = ctx.enter_context(tc.tile_pool(name="raws", bufs=14))
+        stage = ctx.enter_context(tc.tile_pool(name="stage", bufs=4))
+        small = ctx.enter_context(tc.tile_pool(name="small", bufs=2))
+        acc = ctx.enter_context(tc.psum_pool(name="acc", bufs=8))
+
+        offsets = keep.tile([P, SLOTS // 16], U16, name="offsets")
+        window = keep.tile([P, T], F32, name="window")
+        nc.vector.memset(window[:], 0.0)
+
+        x_raw = {}
+        w_raw = {}
+        w2_raw = {}
+        gates = {}
+        for g in range(PASSES):
+            for half in range(2):
+                x_raw[g, half] = raws.tile([P, J, 512], F32, name="raw")
+                nc.sync.dma_start(out=x_raw[g, half][:], in_=xT_view[g, :, :, half * HALF_T : (half + 1) * HALF_T])
+                if g == 0 and half == 0:
+                    nc.sync.dma_start(offsets[:], offs)
+        for e in range(E):
+            for m, g in ((0, 0), (1, 0), (0, 1), (1, 1), (0, 2), (1, 2)):
+                if (e, m, g) == (1, 1, 2):
+                    for q in range(2):
+                        w_raw[e, m, g, q] = raws.tile([P, J, 256], F32, name="raw_half", bufs=2)
+                        nc.sync.dma_start(
+                            out=w_raw[e, m, g, q][:], in_=w_views[m][e, g, :, :, q * 256 : (q + 1) * 256]
+                        )
+                else:
+                    w_raw[e, m, g] = raws.tile([P, J, 512], F32, name="raw")
+                    nc.sync.dma_start(out=w_raw[e, m, g][:], in_=w_views[m][e, g])
+            w2_raw[e] = keep.tile([P, J, N], F32, name=f"w2_raw{e}")
+            nc.sync.dma_start(out=w2_raw[e][:], in_=w2_view[e])
+            gates[e] = keep.tile([P, C], F32, name=f"gates{e}")
+            nc.sync.dma_start(out=gates[e][:], in_=gate[:, e * C : (e + 1) * C])
+
+        x_words = {}
+        s_words = {}
+        x_bytes = keep.tile([P, T], U8, name="x_bytes", align_bytes=64)
+        s_bytes = keep.tile([P, SLOTS], U8, name="s_bytes", align_bytes=64)
+        for g in range(PASSES):
+            x_words[g] = keep.tile([P, T], U32, name=f"x_words{g}", align_bytes=64)
+            s_words[g] = keep.tile([P, SLOTS], U32, name=f"s_words{g}", align_bytes=64)
+            for half in range(2):
+                src = x_raw[g, half][:].rearrange("p j (c i) -> p c j i", i=4)
+                grouped = stage.tile([P, 512 * J], BF16, name="grouped", align_bytes=64)
+                dst = grouped[:].rearrange("p (c i j) -> p c j i", i=4, j=J)
+                nc.scalar.copy(dst[:, : X_CUT // 4], src[:, : X_CUT // 4])
+                nc.vector.tensor_copy(dst[:, X_CUT // 4 :], src[:, X_CUT // 4 :])
+                cols = slice(half * HALF_T, (half + 1) * HALF_T)
+                nc.vector.quantize_mx(
+                    out=x_words[g][:, cols].bitcast(FP8X4), scales=x_bytes[4 * g :, cols], in_=grouped[:]
+                )
+            nc.vector.tensor_copy(s_words[g][:], x_words[g][:].indirect(offsets[:]))
+        nc.vector.tensor_copy(s_bytes[:], x_bytes[:].indirect(offsets[:]))
+
+        w_words = {}
+        w_bytes = {}
+        for e in range(E):
+            gated = small.tile([P, 4, C], F32, name="gated")
+            banks = {}
+            for m, g in ((0, 0), (1, 0), (0, 1), (1, 1), (0, 2), (1, 2)):
+                words = keep.tile([P, H], U32, name=f"w_words{e}{m}{g}", align_bytes=64)
+                scales = keep.tile([P, H], U8, name=f"w_bytes{e}{m}{g}", align_bytes=64)
+                w_words[m, g], w_bytes[m, g] = words, scales
+                grouped = stage.tile([P, 512 * J], BF16, name="grouped", align_bytes=64)
+                dst = grouped[:].rearrange("p (t m j) -> p m t j", t=4, j=J)
+                if (e, m, g) == (1, 1, 2):
+                    for q in range(2):
+                        src = w_raw[e, m, g, q][:].rearrange("p j (m t) -> p m t j", t=4)
+                        m0, m1, m2 = 64 * q, 64 * q + L_CUT, 64 * (q + 1)
+                        nc.scalar.copy(dst[:, m0:m1], src[:, :L_CUT])
+                        nc.vector.tensor_copy(dst[:, m1:m2], src[:, L_CUT:])
+                        for t in range(4):
+                            cols = slice(128 * t + m0, 128 * t + m2)
+                            nc.vector.quantize_mx(
+                                out=words[:, cols].bitcast(FP8X4),
+                                scales=scales[:, cols],
+                                in_=grouped[:, 4 * cols.start : 4 * cols.stop],
+                            )
+                else:
+                    src = w_raw[e, m, g][:].rearrange("p j (m t) -> p m t j", t=4)
+                    nc.scalar.copy(dst[:, :W_CUT], src[:, :W_CUT])
+                    nc.vector.tensor_copy(dst[:, W_CUT:], src[:, W_CUT:])
+                    nc.vector.quantize_mx(out=words[:].bitcast(FP8X4), scales=scales[:], in_=grouped[:])
+                for t in range(4):
+                    cols = slice(128 * t, 128 * (t + 1))
+                    if g == 0:
+                        banks[m, t] = acc.tile([P, C], F32, name="bank")
+                    nc.tensor.matmul_mx(
+                        out=banks[m, t][:],
+                        lhsT=words[:, cols].bitcast(FP8X4),
+                        lhsT_scale=scales[:, cols],
+                        rhs=s_words[g][:, e * C : (e + 1) * C].bitcast(FP8X4),
+                        rhs_scale=s_bytes[4 * g :, e * C : (e + 1) * C],
+                        start=(g == 0),
+                        stop=(g == PASSES - 1),
+                    )
+                    if m == 0 and g == PASSES - 1:
+                        nc.scalar.activation(gated[:, t, :], banks[m, t][:], RELU)
+
+            w2_grouped = small.tile([P, N * J], BF16, name="w2_grouped", align_bytes=64)
+            w2_words = small.tile([P, N], U32, name="w2_words", align_bytes=64)
+            w2_bytes = small.tile([P, N], U8, name="w2_bytes", align_bytes=64)
+            nc.scalar.copy(
+                w2_grouped[:].rearrange("p (c i j) -> p c j i", i=4, j=J),
+                w2_raw[e][:].rearrange("p j (c i) -> p c j i", i=4),
+            )
+            nc.vector.quantize_mx(out=w2_words[:].bitcast(FP8X4), scales=w2_bytes[:], in_=w2_grouped[:])
+            product = small.tile([P, 4, C], BF16, name="product")
+            for t in range(4):
+                nc.vector.tensor_tensor(product[:, t, :], banks[1, t][:], gated[:, t, :], MULT)
+            for b in (1, 0):
+                slots = slice(e * C + b * GROUP, e * C + (b + 1) * GROUP)
+                h = small.tile([P, GROUP, 4], BF16, name="h", align_bytes=64)
+                interleave = nc.scalar.copy if b == 0 else nc.vector.tensor_copy
+                interleave(
+                    h[:].rearrange("p (c i) t -> p c t i", i=4),
+                    product[:, :, b * GROUP : (b + 1) * GROUP].rearrange("p t (c i) -> p c t i", i=4),
+                )
+                h_words = small.tile([P, GROUP], U32, name="h_words", align_bytes=64)
+                h_bytes = small.tile([P, GROUP], U8, name="h_bytes", align_bytes=64)
+                nc.vector.quantize_mx(
+                    out=h_words[:].bitcast(FP8X4), scales=h_bytes[:], in_=h[:].rearrange("p n t -> p (n t)")
+                )
+                y_bank = acc.tile([P, GROUP], F32, name="bank")
+                nc.tensor.matmul_mx(
+                    out=y_bank[:],
+                    lhsT=w2_words[:].bitcast(FP8X4),
+                    lhsT_scale=w2_bytes[:],
+                    rhs=h_words[:].bitcast(FP8X4),
+                    rhs_scale=h_bytes[:],
+                    start=True,
+                    stop=True,
+                )
+                y = small.tile([P, GROUP], F32, name="y")
+                nc.scalar.copy(y[:], y_bank[:])
+                nc.vector.tensor_tensor(
+                    window[:].indirect(offsets[:, slots.start // 16 : slots.stop // 16]),
+                    y[:],
+                    gates[e][:, b * GROUP : (b + 1) * GROUP],
+                    MULT,
+                )
+        nc.sync.dma_start(out=out, in_=window[:])

@@ -20,24 +20,40 @@ PASS = P * J
 PASSES = K // PASS
 SLOTS = E * C
 HALF_T = T // 2
-GROUP = 128
+QUAD = 4
 
-X_CUT = 384
-W_CUT = 64
-L_CUT = 24
+X_CUT = 128
+L_CUT = 20
+W_CUT = 16
+CHUNKS = [(m, g) for g in range(PASSES) for m in range(2)]
+LAST = (E - 1, 1, PASSES - 1)
+PARTS = (1, 2)
 
 
 def tile_routed_moe_kernel(tc, xT, w1, w3, w2, gate, offs, out):
     nc = tc.nc
     xT_view = xT.rearrange("(g p j) n -> g p j n", p=P, j=J)
     w_views = [w.rearrange("e (g p j) n -> e g p j n", p=P, j=J) for w in (w1, w3)]
-    w2_view = w2.rearrange("e (p j) n -> e p j n", j=J)
+    w2_view = w2.rearrange("e (v t r) n -> e r v t n", t=QUAD, r=QUAD)
+
+    def token_source(ap):
+        return ap.rearrange("p j (c i) -> p c j i", i=QUAD)
+
+    def token_target(ap):
+        return ap.rearrange("p (c i j) -> p c j i", i=QUAD, j=J)
+
+    def weight_source(ap):
+        return ap.rearrange("p j (v t r) -> p t v j r", t=QUAD, r=QUAD)
+
+    def weight_target(ap):
+        return ap.rearrange("p (t v r j) -> p t v j r", t=QUAD, r=QUAD, j=J)
+
     with ExitStack() as ctx:
         keep = ctx.enter_context(tc.tile_pool(name="keep", bufs=1))
-        raws = ctx.enter_context(tc.tile_pool(name="raws", bufs=14))
-        stage = ctx.enter_context(tc.tile_pool(name="stage", bufs=4))
+        raws = ctx.enter_context(tc.tile_pool(name="raws", bufs=8))
+        stage = ctx.enter_context(tc.tile_pool(name="stage", bufs=3))
         small = ctx.enter_context(tc.tile_pool(name="small", bufs=2))
-        acc = ctx.enter_context(tc.psum_pool(name="acc", bufs=8))
+        psum = ctx.enter_context(tc.psum_pool(name="psum", bufs=8))
 
         offsets = keep.tile([P, SLOTS // 16], U16, name="offsets")
         window = keep.tile([P, T], F32, name="window")
@@ -48,24 +64,32 @@ def tile_routed_moe_kernel(tc, xT, w1, w3, w2, gate, offs, out):
         w2_raw = {}
         gates = {}
         for g in range(PASSES):
-            for half in range(2):
-                x_raw[g, half] = raws.tile([P, J, 512], F32, name="raw")
-                nc.sync.dma_start(out=x_raw[g, half][:], in_=xT_view[g, :, :, half * HALF_T : (half + 1) * HALF_T])
-                if g == 0 and half == 0:
-                    nc.sync.dma_start(offsets[:], offs)
+            if g <= 0:
+                for half in range(2):
+                    tile = raws.tile([P, J, HALF_T], F32, name="raw")
+                    nc.sync.dma_start(out=tile[:], in_=xT_view[g, :, :, half * HALF_T : (half + 1) * HALF_T])
+                    x_raw[g, half] = tile[:]
+            else:
+                tile = raws.tile([P, J, T], F32, name="x_raw", bufs=2)
+                nc.sync.dma_start(out=tile[:], in_=xT_view[g])
+                for half in range(2):
+                    x_raw[g, half] = tile[:, :, half * HALF_T : (half + 1) * HALF_T]
+            if g == 0:
+                nc.sync.dma_start(offsets[:], offs)
         for e in range(E):
-            for m, g in ((0, 0), (1, 0), (0, 1), (1, 1), (0, 2), (1, 2)):
-                if (e, m, g) == (1, 1, 2):
+            for m, g in CHUNKS:
+                if (e, m, g) == LAST:
                     for q in range(2):
-                        w_raw[e, m, g, q] = raws.tile([P, J, 256], F32, name="raw_half", bufs=2)
-                        nc.sync.dma_start(
-                            out=w_raw[e, m, g, q][:], in_=w_views[m][e, g, :, :, q * 256 : (q + 1) * 256]
-                        )
+                        tile = raws.tile([P, J, H // 2], F32, name="raw_half", bufs=2)
+                        nc.sync.dma_start(out=tile[:], in_=w_views[m][e, g, :, :, q * H // 2 : (q + 1) * H // 2])
+                        w_raw[e, m, g, q] = tile
                 else:
-                    w_raw[e, m, g] = raws.tile([P, J, 512], F32, name="raw")
-                    nc.sync.dma_start(out=w_raw[e, m, g][:], in_=w_views[m][e, g])
+                    tile = raws.tile([P, J, H], F32, name="raw")
+                    nc.sync.dma_start(out=tile[:], in_=w_views[m][e, g])
+                    w_raw[e, m, g] = tile
             w2_raw[e] = keep.tile([P, J, N], F32, name=f"w2_raw{e}")
-            nc.sync.dma_start(out=w2_raw[e][:], in_=w2_view[e])
+            for r in range(QUAD):
+                nc.sync.dma_start(out=w2_raw[e][r:P:QUAD], in_=w2_view[e, r])
             gates[e] = keep.tile([P, C], F32, name=f"gates{e}")
             nc.sync.dma_start(out=gates[e][:], in_=gate[:, e * C : (e + 1) * C])
 
@@ -76,52 +100,44 @@ def tile_routed_moe_kernel(tc, xT, w1, w3, w2, gate, offs, out):
         for g in range(PASSES):
             x_words[g] = keep.tile([P, T], U32, name=f"x_words{g}", align_bytes=64)
             s_words[g] = keep.tile([P, SLOTS], U32, name=f"s_words{g}", align_bytes=64)
+            grouped = stage.tile([P, T * J], BF16, name="grouped", align_bytes=64, bufs=2)
+            target = token_target(grouped[:])
+            first, second = token_source(x_raw[g, 0]), token_source(x_raw[g, 1])
+            middle, cut = HALF_T // QUAD, X_CUT // QUAD
+            nc.scalar.copy(target[:, :middle], first)
+            nc.scalar.copy(target[:, middle : middle + cut], second[:, :cut])
+            nc.vector.tensor_copy(target[:, middle + cut :], second[:, cut:])
             for half in range(2):
-                src = x_raw[g, half][:].rearrange("p j (c i) -> p c j i", i=4)
-                grouped = stage.tile([P, 512 * J], BF16, name="grouped", align_bytes=64)
-                dst = grouped[:].rearrange("p (c i j) -> p c j i", i=4, j=J)
-                nc.scalar.copy(dst[:, : X_CUT // 4], src[:, : X_CUT // 4])
-                nc.vector.tensor_copy(dst[:, X_CUT // 4 :], src[:, X_CUT // 4 :])
                 cols = slice(half * HALF_T, (half + 1) * HALF_T)
                 nc.vector.quantize_mx(
-                    out=x_words[g][:, cols].bitcast(FP8X4), scales=x_bytes[4 * g :, cols], in_=grouped[:]
+                    out=x_words[g][:, cols].bitcast(FP8X4),
+                    scales=x_bytes[4 * g :, cols],
+                    in_=grouped[:, J * cols.start : J * cols.stop],
                 )
             nc.vector.tensor_copy(s_words[g][:], x_words[g][:].indirect(offsets[:]))
         nc.vector.tensor_copy(s_bytes[:], x_bytes[:].indirect(offsets[:]))
 
-        w_words = {}
-        w_bytes = {}
         for e in range(E):
-            gated = small.tile([P, 4, C], F32, name="gated")
             banks = {}
-            for m, g in ((0, 0), (1, 0), (0, 1), (1, 1), (0, 2), (1, 2)):
+            gated = small.tile([P, 4, C], F32, name="gated")
+            for m, g in CHUNKS:
                 words = keep.tile([P, H], U32, name=f"w_words{e}{m}{g}", align_bytes=64)
                 scales = keep.tile([P, H], U8, name=f"w_bytes{e}{m}{g}", align_bytes=64)
-                w_words[m, g], w_bytes[m, g] = words, scales
-                grouped = stage.tile([P, 512 * J], BF16, name="grouped", align_bytes=64)
-                dst = grouped[:].rearrange("p (t m j) -> p m t j", t=4, j=J)
-                if (e, m, g) == (1, 1, 2):
-                    for q in range(2):
-                        src = w_raw[e, m, g, q][:].rearrange("p j (m t) -> p m t j", t=4)
-                        m0, m1, m2 = 64 * q, 64 * q + L_CUT, 64 * (q + 1)
-                        nc.scalar.copy(dst[:, m0:m1], src[:, :L_CUT])
-                        nc.vector.tensor_copy(dst[:, m1:m2], src[:, L_CUT:])
-                        for t in range(4):
-                            cols = slice(128 * t + m0, 128 * t + m2)
-                            nc.vector.quantize_mx(
-                                out=words[:, cols].bitcast(FP8X4),
-                                scales=scales[:, cols],
-                                in_=grouped[:, 4 * cols.start : 4 * cols.stop],
-                            )
+                grouped = stage.tile([P, H * J], BF16, name="w_grouped", align_bytes=64, bufs=5)
+                target = weight_target(grouped[:])
+                if (e, m, g) == LAST:
+                    pieces = [(w_raw[e, m, g, q], 16 * q, 16 * q + L_CUT // 4, 16 * (q + 1)) for q in range(2)]
                 else:
-                    src = w_raw[e, m, g][:].rearrange("p j (m t) -> p m t j", t=4)
-                    nc.scalar.copy(dst[:, :W_CUT], src[:, :W_CUT])
-                    nc.vector.tensor_copy(dst[:, W_CUT:], src[:, W_CUT:])
-                    nc.vector.quantize_mx(out=words[:].bitcast(FP8X4), scales=scales[:], in_=grouped[:])
+                    pieces = [(w_raw[e, m, g], 0, W_CUT, 32)]
+                for raw, v0, v1, v2 in pieces:
+                    source = weight_source(raw[:])
+                    nc.scalar.copy(target[:, :, v0:v1], source[:, :, : v1 - v0])
+                    nc.vector.tensor_copy(target[:, :, v1:v2], source[:, :, v1 - v0 :])
+                nc.vector.quantize_mx(out=words[:].bitcast(FP8X4), scales=scales[:], in_=grouped[:])
                 for t in range(4):
                     cols = slice(128 * t, 128 * (t + 1))
                     if g == 0:
-                        banks[m, t] = acc.tile([P, C], F32, name="bank")
+                        banks[m, t] = psum.tile([P, C], F32, name="bank")
                     nc.tensor.matmul_mx(
                         out=banks[m, t][:],
                         lhsT=words[:, cols].bitcast(FP8X4),
@@ -137,28 +153,21 @@ def tile_routed_moe_kernel(tc, xT, w1, w3, w2, gate, offs, out):
             w2_grouped = small.tile([P, N * J], BF16, name="w2_grouped", align_bytes=64)
             w2_words = small.tile([P, N], U32, name="w2_words", align_bytes=64)
             w2_bytes = small.tile([P, N], U8, name="w2_bytes", align_bytes=64)
-            nc.scalar.copy(
-                w2_grouped[:].rearrange("p (c i j) -> p c j i", i=4, j=J),
-                w2_raw[e][:].rearrange("p j (c i) -> p c j i", i=4),
-            )
+            nc.scalar.copy(token_target(w2_grouped[:]), token_source(w2_raw[e][:]))
             nc.vector.quantize_mx(out=w2_words[:].bitcast(FP8X4), scales=w2_bytes[:], in_=w2_grouped[:])
+
             product = small.tile([P, 4, C], BF16, name="product")
             for t in range(4):
                 nc.vector.tensor_tensor(product[:, t, :], banks[1, t][:], gated[:, t, :], MULT)
-            for b in (1, 0):
-                slots = slice(e * C + b * GROUP, e * C + (b + 1) * GROUP)
-                h = small.tile([P, GROUP, 4], BF16, name="h", align_bytes=64)
-                interleave = nc.scalar.copy if b == 0 else nc.vector.tensor_copy
-                interleave(
-                    h[:].rearrange("p (c i) t -> p c t i", i=4),
-                    product[:, :, b * GROUP : (b + 1) * GROUP].rearrange("p t (c i) -> p c t i", i=4),
-                )
-                h_words = small.tile([P, GROUP], U32, name="h_words", align_bytes=64)
-                h_bytes = small.tile([P, GROUP], U8, name="h_bytes", align_bytes=64)
-                nc.vector.quantize_mx(
-                    out=h_words[:].bitcast(FP8X4), scales=h_bytes[:], in_=h[:].rearrange("p n t -> p (n t)")
-                )
-                y_bank = acc.tile([P, GROUP], F32, name="bank")
+            size = C // PARTS[e]
+            for b in range(PARTS[e]):
+                part = slice(b * size, (b + 1) * size)
+                h = small.tile([P, size * J], BF16, name="h", align_bytes=64)
+                nc.vector.tensor_copy(token_target(h[:]), token_source(product[:, :, part]))
+                h_words = small.tile([P, size], U32, name="h_words", align_bytes=64)
+                h_bytes = small.tile([P, size], U8, name="h_bytes", align_bytes=64)
+                nc.vector.quantize_mx(out=h_words[:].bitcast(FP8X4), scales=h_bytes[:], in_=h[:])
+                y_bank = psum.tile([P, size], F32, name="bank")
                 nc.tensor.matmul_mx(
                     out=y_bank[:],
                     lhsT=w2_words[:].bitcast(FP8X4),
@@ -168,12 +177,10 @@ def tile_routed_moe_kernel(tc, xT, w1, w3, w2, gate, offs, out):
                     start=True,
                     stop=True,
                 )
-                y = small.tile([P, GROUP], F32, name="y")
+                y = small.tile([P, size], F32, name="y")
                 nc.scalar.copy(y[:], y_bank[:])
+                first = (e * C + part.start) // 16
                 nc.vector.tensor_tensor(
-                    window[:].indirect(offsets[:, slots.start // 16 : slots.stop // 16]),
-                    y[:],
-                    gates[e][:, b * GROUP : (b + 1) * GROUP],
-                    MULT,
+                    window[:].indirect(offsets[:, first : first + size // 16]), y[:], gates[e][:, part], MULT
                 )
         nc.sync.dma_start(out=out, in_=window[:])

@@ -22,9 +22,9 @@ SLOTS = E * C
 HALF_T = T // 2
 QUAD = 4
 
-X_CUT = 128
-L_CUT = 20
-W_CUT = 16
+X_CUT = 512
+L_CUT = 24
+W_CUT = 20
 CHUNKS = [(m, g) for g in range(PASSES) for m in range(2)]
 LAST = (E - 1, 1, PASSES - 1)
 PARTS = (1, 2)
@@ -50,7 +50,7 @@ def tile_routed_moe_kernel(tc, xT, w1, w3, w2, gate, offs, out):
 
     with ExitStack() as ctx:
         keep = ctx.enter_context(tc.tile_pool(name="keep", bufs=1))
-        raws = ctx.enter_context(tc.tile_pool(name="raws", bufs=8))
+        raws = ctx.enter_context(tc.tile_pool(name="raws", bufs=7))
         stage = ctx.enter_context(tc.tile_pool(name="stage", bufs=3))
         small = ctx.enter_context(tc.tile_pool(name="small", bufs=2))
         psum = ctx.enter_context(tc.psum_pool(name="psum", bufs=8))
@@ -64,20 +64,26 @@ def tile_routed_moe_kernel(tc, xT, w1, w3, w2, gate, offs, out):
         w2_raw = {}
         gates = {}
         for g in range(PASSES):
-            if g <= 0:
-                for half in range(2):
-                    tile = raws.tile([P, J, HALF_T], F32, name="raw")
-                    nc.sync.dma_start(out=tile[:], in_=xT_view[g, :, :, half * HALF_T : (half + 1) * HALF_T])
-                    x_raw[g, half] = tile[:]
-            else:
-                tile = raws.tile([P, J, T], F32, name="x_raw", bufs=2)
-                nc.sync.dma_start(out=tile[:], in_=xT_view[g])
-                for half in range(2):
-                    x_raw[g, half] = tile[:, :, half * HALF_T : (half + 1) * HALF_T]
+            x_raw[g] = raws.tile([P, J, T], F32, name="x_raw", bufs=3)
+            nc.sync.dma_start(out=x_raw[g][:], in_=xT_view[g])
             if g == 0:
                 nc.sync.dma_start(offsets[:], offs)
+        def load_w2(e):
+            w2_raw[e] = keep.tile([P, J, N], F32, name=f"w2_raw{e}")
+            for r in range(QUAD):
+                nc.sync.dma_start(out=w2_raw[e][r:P:QUAD], in_=w2_view[e, r])
+
+        def load_gate(e):
+            gates[e] = keep.tile([P, C], F32, name=f"gates{e}")
+            nc.sync.dma_start(out=gates[e][:], in_=gate[:, e * C : (e + 1) * C])
+
         for e in range(E):
-            for m, g in CHUNKS:
+            for i in range(len(CHUNKS)):
+                m, g = CHUNKS[i]
+                if (e, i) == (1, 1):
+                    load_w2(0)
+                if (e, i) == (1, 3):
+                    load_gate(0)
                 if (e, m, g) == LAST:
                     for q in range(2):
                         tile = raws.tile([P, J, H // 2], F32, name="raw_half", bufs=2)
@@ -87,11 +93,8 @@ def tile_routed_moe_kernel(tc, xT, w1, w3, w2, gate, offs, out):
                     tile = raws.tile([P, J, H], F32, name="raw")
                     nc.sync.dma_start(out=tile[:], in_=w_views[m][e, g])
                     w_raw[e, m, g] = tile
-            w2_raw[e] = keep.tile([P, J, N], F32, name=f"w2_raw{e}")
-            for r in range(QUAD):
-                nc.sync.dma_start(out=w2_raw[e][r:P:QUAD], in_=w2_view[e, r])
-            gates[e] = keep.tile([P, C], F32, name=f"gates{e}")
-            nc.sync.dma_start(out=gates[e][:], in_=gate[:, e * C : (e + 1) * C])
+        load_w2(E - 1)
+        load_gate(E - 1)
 
         x_words = {}
         s_words = {}
@@ -102,11 +105,9 @@ def tile_routed_moe_kernel(tc, xT, w1, w3, w2, gate, offs, out):
             s_words[g] = keep.tile([P, SLOTS], U32, name=f"s_words{g}", align_bytes=64)
             grouped = stage.tile([P, T * J], BF16, name="grouped", align_bytes=64, bufs=2)
             target = token_target(grouped[:])
-            first, second = token_source(x_raw[g, 0]), token_source(x_raw[g, 1])
-            middle, cut = HALF_T // QUAD, X_CUT // QUAD
-            nc.scalar.copy(target[:, :middle], first)
-            nc.scalar.copy(target[:, middle : middle + cut], second[:, :cut])
-            nc.vector.tensor_copy(target[:, middle + cut :], second[:, cut:])
+            source = token_source(x_raw[g][:])
+            nc.scalar.copy(target[:, : X_CUT // QUAD], source[:, : X_CUT // QUAD])
+            nc.vector.tensor_copy(target[:, X_CUT // QUAD :], source[:, X_CUT // QUAD :])
             for half in range(2):
                 cols = slice(half * HALF_T, (half + 1) * HALF_T)
                 nc.vector.quantize_mx(
@@ -163,7 +164,8 @@ def tile_routed_moe_kernel(tc, xT, w1, w3, w2, gate, offs, out):
             for b in range(PARTS[e]):
                 part = slice(b * size, (b + 1) * size)
                 h = small.tile([P, size * J], BF16, name="h", align_bytes=64)
-                nc.vector.tensor_copy(token_target(h[:]), token_source(product[:, :, part]))
+                interleave = nc.vector.tensor_copy if b == 0 else nc.scalar.copy
+                interleave(token_target(h[:]), token_source(product[:, :, part]))
                 h_words = small.tile([P, size], U32, name="h_words", align_bytes=64)
                 h_bytes = small.tile([P, size], U8, name="h_bytes", align_bytes=64)
                 nc.vector.quantize_mx(out=h_words[:].bitcast(FP8X4), scales=h_bytes[:], in_=h[:])

from contextlib import ExitStack

import concourse.mybir as mybir

K, T, E, C, H, N = 1536, 1024, 2, 256, 512, 128
FLOPS = 2 * E * C * (2 * K * H + H * N)

F32 = mybir.dt.float32
BF16 = mybir.dt.bfloat16
U32 = mybir.dt.uint32
U16 = mybir.dt.uint16
U8 = mybir.dt.uint8
FP8X4 = mybir.dt.float8_e4m3fn_x4
MULT = mybir.AluOpType.mult
RELU = mybir.ActivationFunctionType.Relu

P = 128
J = 4
PASS = P * J
PASSES = K // PASS
SLOTS = E * C
HALF_T = T // 2
QUAD = 4

X_CUT = 512
L_CUT = 24
W_CUT = 20
CHUNKS = [(m, g) for g in range(PASSES) for m in range(2)]
LAST = (E - 1, 1, PASSES - 1)
PARTS = (1, 2)


def tile_routed_moe_kernel(tc, xT, w1, w3, w2, gate, offs, out):
    nc = tc.nc
    xT_view = xT.rearrange("(g p j) n -> g p j n", p=P, j=J)
    w_views = [w.rearrange("e (g p j) n -> e g p j n", p=P, j=J) for w in (w1, w3)]
    w2_view = w2.rearrange("e (v t r) n -> e r v t n", t=QUAD, r=QUAD)

    def token_source(ap):
        return ap.rearrange("p j (c i) -> p c j i", i=QUAD)

    def token_target(ap):
        return ap.rearrange("p (c i j) -> p c j i", i=QUAD, j=J)

    def weight_source(ap):
        return ap.rearrange("p j (v t r) -> p t v j r", t=QUAD, r=QUAD)

    def weight_target(ap):
        return ap.rearrange("p (t v r j) -> p t v j r", t=QUAD, r=QUAD, j=J)

    with ExitStack() as ctx:
        keep = ctx.enter_context(tc.tile_pool(name="keep", bufs=1))
        raws = ctx.enter_context(tc.tile_pool(name="raws", bufs=7))
        stage = ctx.enter_context(tc.tile_pool(name="stage", bufs=3))
        small = ctx.enter_context(tc.tile_pool(name="small", bufs=2))
        psum = ctx.enter_context(tc.psum_pool(name="psum", bufs=8))

        offsets = keep.tile([P, SLOTS // 16], U16, name="offsets")
        window = keep.tile([P, T], F32, name="window")
        nc.vector.memset(window[:], 0.0)

        x_raw = {}
        w_raw = {}
        w2_raw = {}
        gates = {}
        for g in range(PASSES):
            x_raw[g] = raws.tile([P, J, T], F32, name="x_raw", bufs=3)
            nc.sync.dma_start(out=x_raw[g][:], in_=xT_view[g])
            if g == 0:
                nc.sync.dma_start(offsets[:], offs)
        def load_w2(e):
            w2_raw[e] = keep.tile([P, J, N], F32, name=f"w2_raw{e}")
            for r in range(QUAD):
                nc.sync.dma_start(out=w2_raw[e][r:P:QUAD], in_=w2_view[e, r])

        def load_gate(e):
            gates[e] = keep.tile([P, C], F32, name=f"gates{e}")
            nc.sync.dma_start(out=gates[e][:], in_=gate[:, e * C : (e + 1) * C])

        for e in range(E):
            for i in range(len(CHUNKS)):
                m, g = CHUNKS[i]
                if (e, i) == (1, 1):
                    load_w2(0)
                if (e, i) == (1, 3):
                    load_gate(0)
                if (e, m, g) == LAST:
                    for q in range(2):
                        tile = raws.tile([P, J, H // 2], F32, name="raw_half", bufs=2)
                        nc.sync.dma_start(out=tile[:], in_=w_views[m][e, g, :, :, q * H // 2 : (q + 1) * H // 2])
                        w_raw[e, m, g, q] = tile
                else:
                    tile = raws.tile([P, J, H], F32, name="raw")
                    nc.sync.dma_start(out=tile[:], in_=w_views[m][e, g])
                    w_raw[e, m, g] = tile
        load_w2(E - 1)
        load_gate(E - 1)

        x_words = {}
        s_words = {}
        x_bytes = keep.tile([P, T], U8, name="x_bytes", align_bytes=64)
        s_bytes = keep.tile([P, SLOTS], U8, name="s_bytes", align_bytes=64)
        for g in range(PASSES):
            x_words[g] = keep.tile([P, T], U32, name=f"x_words{g}", align_bytes=64)
            s_words[g] = keep.tile([P, SLOTS], U32, name=f"s_words{g}", align_bytes=64)
            grouped = stage.tile([P, T * J], BF16, name="grouped", align_bytes=64, bufs=2)
            target = token_target(grouped[:])
            source = token_source(x_raw[g][:])
            nc.scalar.copy(target[:, : X_CUT // QUAD], source[:, : X_CUT // QUAD])
            nc.vector.tensor_copy(target[:, X_CUT // QUAD :], source[:, X_CUT // QUAD :])
            for half in range(2):
                cols = slice(half * HALF_T, (half + 1) * HALF_T)
                nc.vector.quantize_mx(
                    out=x_words[g][:, cols].bitcast(FP8X4),
                    scales=x_bytes[4 * g :, cols],
                    in_=grouped[:, J * cols.start : J * cols.stop],
                )
            nc.vector.tensor_copy(s_words[g][:], x_words[g][:].indirect(offsets[:]))
        nc.vector.tensor_copy(s_bytes[:], x_bytes[:].indirect(offsets[:]))

        for e in range(E):
            banks = {}
            gated = small.tile([P, 4, C], F32, name="gated")
            for m, g in CHUNKS:
                words = keep.tile([P, H], U32, name=f"w_words{e}{m}{g}", align_bytes=64)
                scales = keep.tile([P, H], U8, name=f"w_bytes{e}{m}{g}", align_bytes=64)
                grouped = stage.tile([P, H * J], BF16, name="w_grouped", align_bytes=64, bufs=5)
                target = weight_target(grouped[:])
                if (e, m, g) == LAST:
                    pieces = [(w_raw[e, m, g, q], 16 * q, 16 * q + L_CUT // 4, 16 * (q + 1)) for q in range(2)]
                else:
                    pieces = [(w_raw[e, m, g], 0, W_CUT, 32)]
                for raw, v0, v1, v2 in pieces:
                    source = weight_source(raw[:])
                    nc.scalar.copy(target[:, :, v0:v1], source[:, :, : v1 - v0])
                    nc.vector.tensor_copy(target[:, :, v1:v2], source[:, :, v1 - v0 :])
                nc.vector.quantize_mx(out=words[:].bitcast(FP8X4), scales=scales[:], in_=grouped[:])
                for t in range(4):
                    cols = slice(128 * t, 128 * (t + 1))
                    if g == 0:
                        banks[m, t] = psum.tile([P, C], F32, name="bank")
                    nc.tensor.matmul_mx(
                        out=banks[m, t][:],
                        lhsT=words[:, cols].bitcast(FP8X4),
                        lhsT_scale=scales[:, cols],
                        rhs=s_words[g][:, e * C : (e + 1) * C].bitcast(FP8X4),
                        rhs_scale=s_bytes[4 * g :, e * C : (e + 1) * C],
                        start=(g == 0),
                        stop=(g == PASSES - 1),
                    )
                    if m == 0 and g == PASSES - 1:
                        nc.scalar.activation(gated[:, t, :], banks[m, t][:], RELU)

            w2_grouped = small.tile([P, N * J], BF16, name="w2_grouped", align_bytes=64)
            w2_words = small.tile([P, N], U32, name="w2_words", align_bytes=64)
            w2_bytes = small.tile([P, N], U8, name="w2_bytes", align_bytes=64)
            nc.scalar.copy(token_target(w2_grouped[:]), token_source(w2_raw[e][:]))
            nc.vector.quantize_mx(out=w2_words[:].bitcast(FP8X4), scales=w2_bytes[:], in_=w2_grouped[:])

            product = small.tile([P, 4, C], BF16, name="product")
            for t in range(4):
                nc.vector.tensor_tensor(product[:, t, :], banks[1, t][:], gated[:, t, :], MULT)
            size = C // PARTS[e]
            for b in range(PARTS[e]):
                part = slice(b * size, (b + 1) * size)
                h = small.tile([P, size * J], BF16, name="h", align_bytes=64)
                interleave = nc.vector.tensor_copy if b == 0 else nc.scalar.copy
                interleave(token_target(h[:]), token_source(product[:, :, part]))
                h_words = small.tile([P, size], U32, name="h_words", align_bytes=64)
                h_bytes = small.tile([P, size], U8, name="h_bytes", align_bytes=64)
                nc.vector.quantize_mx(out=h_words[:].bitcast(FP8X4), scales=h_bytes[:], in_=h[:])
                y_bank = psum.tile([P, size], F32, name="bank")
                nc.tensor.matmul_mx(
                    out=y_bank[:],
                    lhsT=w2_words[:].bitcast(FP8X4),
                    lhsT_scale=w2_bytes[:],
                    rhs=h_words[:].bitcast(FP8X4),
                    rhs_scale=h_bytes[:],
                    start=True,
                    stop=True,
                )
                y = small.tile([P, size], F32, name="y")
                nc.scalar.copy(y[:], y_bank[:])
                first = (e * C + part.start) // 16
                nc.vector.tensor_tensor(
                    window[:].indirect(offsets[:, first : first + size // 16]), y[:], gates[e][:, part], MULT
                )
        nc.sync.dma_start(out=out, in_=window[:])
